import numpy as np
import ml_dtypes


def mxq(x, axis, fmt="e4m3"):
    dtype, down = {"e4m3": (ml_dtypes.float8_e4m3fn, 7), "e5m2": (ml_dtypes.float8_e5m2, 14)}[fmt]
    v = np.moveaxis(np.asarray(x, np.float32).astype(ml_dtypes.bfloat16).astype(np.float64), axis, -1)
    blocks = v.reshape(v.shape[:-1] + (-1, 32))
    amax = np.abs(blocks).max(-1, keepdims=True)
    byte = np.maximum(np.where(amax > 0, np.frexp(amax)[1] - 1 + 127, 0) - down, 1)
    scale = np.exp2(byte - 127.0)
    codes = (blocks / scale).astype(np.float32).astype(dtype).astype(np.float64)
    return np.moveaxis((codes * scale).reshape(v.shape), -1, axis)


WIDE = False


def mx_kscale(k):
    if not WIDE:
        return np.ones(k)
    levels = np.array([10, -10, 5, -5, 0])
    if k % 512:
        return np.exp2(np.random.permutation(np.resize(levels, k // 32))).repeat(32)
    a = np.empty((k // 512, 16))
    for p in range(k // 512):
        a[p, :8] = np.random.permutation(np.resize(levels, 8))
        for g in range(8):
            far = levels[np.abs(levels - a[p, g]) >= 10]
            a[p, g + 8] = far[np.random.randint(len(far))]
    return np.exp2(a.ravel()).repeat(32)


def f64(x):
    return np.asarray(x).astype(np.float64)


def striped(idx):
    return np.tile(idx.reshape(-1, 16).T, (8, 1)).astype(np.uint16)


def unstriped(offs):
    return offs[:16].T.reshape(-1).astype(np.int64)


def gelu(v):
    return 0.5 * v * (1.0 + np.tanh(np.sqrt(2.0 / np.pi) * (v + 0.044715 * v**3)))


K, T, E, C, N = 512, 1024, 8, 256, 128
TOP = 4
PAD = 64


def by_expert(wq, xq):
    return np.concatenate([wq[e].T @ xq[:, e * C:(e + 1) * C] for e in range(E)], axis=1)


def setup_inputs():
    n = np.random.standard_normal
    s = mx_kscale(K)[:, None]
    slot_token = np.empty(E * C, np.int64); pos = np.tile(E * C + np.arange(T) % PAD, (TOP, 1)); taken = np.zeros(T, np.int64)
    liked = np.random.randn(T)
    for e in np.random.permutation(E):
        free = np.flatnonzero(taken < TOP); pick = np.random.permutation(free[np.argsort(-(liked[free] + np.random.gumbel(size=free.size)))[:C]]); slot_token[e * C:(e + 1) * C] = pick
        pos[taken[pick], pick] = e * C + np.arange(C); taken[pick] += 1
    g = np.random.uniform(0.2, 0.8, (TOP, T))
    return {
        "xT": (n((K, T)) * s).astype(np.float32),
        "w": (n((E, K, N)) / np.sqrt(K) / s[None]).astype(np.float32),
        "b": (0.3 * n((N, E))).astype(np.float32),
        "gate": np.stack([np.tile(r, (N, 1)) for r in g]).astype(np.float32),
        "offs": striped(slot_token),
        "pos1": striped(pos[0]),
        "pos2": striped(pos[1]),
        "pos3": striped(pos[2]),
        "pos4": striped(pos[3]),
    }


def reference(xT, w, b, gate, offs, pos1, pos2, pos3, pos4):
    idx = unstriped(offs)
    xq = mxq(f64(xT)[:, idx], 0, "e4m3")
    y = by_expert(mxq(f64(w), 1, "e4m3"), xq)
    y = gelu(y + np.repeat(f64(b), C, axis=1))
    y = np.concatenate([y, np.zeros((N, PAD))], axis=1)
    return sum(f64(gate[r]) * y[:, unstriped(p)] for r, p in enumerate((pos1, pos2, pos3, pos4)))

@@ -1,0 +1,189 @@
+from contextlib import ExitStack
+
+import concourse.mybir as mybir
+from concourse.masks import make_identity
+
+K, T, E, C, N = 512, 1024, 8, 256, 128
+TOP = 4
+PAD = 64
+SLOTS = E * C
+FLOPS = 2 * K * N * SLOTS
+
+F32 = mybir.dt.float32
+BF16 = mybir.dt.bfloat16
+I32 = mybir.dt.int32
+U32 = mybir.dt.uint32
+U16 = mybir.dt.uint16
+U8 = mybir.dt.uint8
+FP8X4 = mybir.dt.float8_e4m3fn_x4
+MULT = mybir.AluOpType.mult
+ADD = mybir.AluOpType.add
+GELU = mybir.ActivationFunctionType.Gelu_apprx_tanh
+
+P = 128
+PACK = 4
+STRIPE = 16
+X_CHUNK = 256
+LAST_VECTOR_SHARE = 160
+WORD_LEAD = 2
+CHUNK = 256
+W_BYTES = PACK * N * 4
+
+
+def interleave(copy, grouped, raw, cols):
+    copy(
+        out=grouped[:, cols, :].rearrange("p (c i) j -> p c j i", i=4),
+        in_=raw[:, :, cols].rearrange("p j (c i) -> p c j i", i=4),
+    )
+
+
+def tile_moe_ecr_lin_gelu_kernel(tc, xT, w, b, gate, offs, pos1, pos2, pos3, pos4, out):
+    nc = tc.nc
+    with ExitStack() as ctx:
+        keep = ctx.enter_context(tc.tile_pool(name="keep", bufs=1))
+        shared = ctx.enter_context(tc.tile_pool(name="shared", bufs=1))
+        psum = ctx.enter_context(tc.psum_pool(name="psum", bufs=1))
+
+        def bank(index, name):
+            return psum.tile([P, 512], F32, name=name, tag="bank%d" % index)
+
+        x_raw = []
+        for c in range(T // X_CHUNK):
+            raw = keep.tile([P, PACK, X_CHUNK], F32, name="x_raw%d" % c)
+            cols = slice(c * X_CHUNK, (c + 1) * X_CHUNK)
+            nc.sync.dma_start(out=raw[:], in_=xT[:, cols].rearrange("(p j) t -> p j t", j=PACK))
+            x_raw.append(raw)
+        offs_sb = keep.tile([P, SLOTS // STRIPE], U16, name="offs_sb")
+        nc.sync.dma_start(offs_sb[:], offs)
+        w_raw = []
+        for e in range(E):
+            raw = shared.tile([P, PACK, N], F32, name="w_raw%d" % e, offset=e * W_BYTES, align_bytes=64)
+            nc.sync.dma_start(out=raw[:], in_=w[e].rearrange("(p j) n -> p j n", j=PACK))
+            w_raw.append(raw)
+            if e == 0:
+                bias = keep.tile([P, E], F32, name="bias")
+                nc.sync.dma_start(out=bias[:], in_=b)
+        pos_sb = []
+        gate_sb = []
+        for r, pos in enumerate((pos1, pos2, pos3, pos4)):
+            lst = keep.tile([P, T // STRIPE], U16, name="pos_sb%d" % r)
+            nc.sync.dma_start(lst[:], pos)
+            pos_sb.append(lst)
+        half = T // 2
+        gate_parts = [(0, TOP - 1, half, half)]
+        gate_parts.extend((0, TOP, c * CHUNK, CHUNK) for c in range(half // CHUNK))
+        gate_parts.append((TOP - 1, TOP, half, half))
+        for r0, r1, t0, width in gate_parts:
+            g = keep.tile([P, r1 - r0, width], F32, name="gate_sb%d_%d" % (r0, t0))
+            nc.sync.dma_start(out=g[:], in_=gate[r0:r1, :, t0 : t0 + width].rearrange("r n t -> n r t"))
+            gate_sb.append(g)
+
+        def gate_of(r, t0, width):
+            for (r0, r1, g0, g_width), g in zip(gate_parts, gate_sb):
+                if r0 <= r < r1 and g0 <= t0 < g0 + g_width:
+                    return g[:, r - r0, t0 - g0 : t0 - g0 + width]
+
+        x_scales = keep.tile([P, T], U8, name="x_scales", align_bytes=64)
+        nc.vector.memset(x_scales[:].bitcast(I32), 0)
+        zeros = keep.tile([P, PAD], F32, name="zeros")
+        nc.vector.memset(zeros[:], 0.0)
+        y = keep.tile([P, SLOTS + PAD], F32, name="y")
+        nc.scalar.activation(y[:, SLOTS:], zeros[:], GELU)
+        ident = keep.tile([P, P], F32, name="ident")
+        make_identity(nc, ident[:])
+
+        x_words = keep.tile([P, T], U32, name="x_words", align_bytes=64)
+        for c, raw in enumerate(x_raw):
+            grouped = keep.tile([P, X_CHUNK, PACK], BF16, name="x_bf%d" % c, align_bytes=64)
+            if c == len(x_raw) - 1:
+                interleave(nc.vector.tensor_copy, grouped, raw, slice(0, LAST_VECTOR_SHARE))
+                interleave(nc.scalar.copy, grouped, raw, slice(LAST_VECTOR_SHARE, X_CHUNK))
+            else:
+                interleave(nc.vector.tensor_copy, grouped, raw, slice(0, X_CHUNK))
+            cols = slice(c * X_CHUNK, (c + 1) * X_CHUNK)
+            nc.vector.quantize_mx(
+                out=x_words[:, cols].bitcast(FP8X4),
+                scales=x_scales[:, cols],
+                in_=grouped[:].rearrange("p t j -> p (t j)"),
+            )
+
+        def slot_offsets(e):
+            return offs_sb[:, e * C // STRIPE : (e + 1) * C // STRIPE]
+
+        def gather_words(e):
+            if e < WORD_LEAD:
+                words = keep.tile([P, C], U32, name="slot_words%d" % e, align_bytes=64)
+            else:
+                words = shared.tile(
+                    [P, C], U32, name="slot_words%d" % e, offset=(e - WORD_LEAD) * W_BYTES, align_bytes=64
+                )
+            nc.vector.tensor_copy(words[:], x_words[:].indirect(slot_offsets(e)))
+            return words
+
+        slot_words = [gather_words(e) for e in range(WORD_LEAD)]
+        for e in range(E):
+            grouped = keep.tile([P, N, PACK], BF16, name="w_bf%d" % e, align_bytes=64)
+            interleave(nc.scalar.copy, grouped, w_raw[e], slice(0, N))
+            w_words = keep.tile([P, N], U32, name="w_words%d" % e, align_bytes=64)
+            w_scales = keep.tile([P, N], U8, name="w_scales%d" % e, align_bytes=64)
+            nc.vector.quantize_mx(
+                out=w_words[:].bitcast(FP8X4),
+                scales=w_scales[:],
+                in_=grouped[:].rearrange("p n j -> p (n j)"),
+            )
+            slot_scales = shared.tile(
+                [P, C], U8, name="slot_scales%d" % e, offset=e * W_BYTES + 4 * C, align_bytes=64
+            )
+            nc.vector.tensor_copy(slot_scales[:], x_scales[:].indirect(slot_offsets(e)))
+            if e + WORD_LEAD < E:
+                slot_words.append(gather_words(e + WORD_LEAD))
+            acc = bank(e, "acc%d" % e)
+            nc.tensor.matmul_mx(
+                out=acc[:, :C],
+                lhsT=w_words[:].bitcast(FP8X4),
+                lhsT_scale=w_scales[:],
+                rhs=slot_words[e][:].bitcast(FP8X4),
+                rhs_scale=slot_scales[:],
+                start=True,
+                stop=True,
+            )
+            nc.scalar.activation(y[:, e * C : (e + 1) * C], acc[:, :C], GELU, bias=bias[:, e : e + 1])
+
+        def weighted(r, t0, width):
+            z = keep.tile([P, width], F32, name="z%d_%d" % (r, t0))
+            offsets = pos_sb[r][:, t0 // STRIPE : (t0 + width) // STRIPE]
+            nc.vector.tensor_tensor(z[:], y[:].indirect(offsets), gate_of(r, t0, width), MULT)
+            return z
+
+        def summed(terms, t0, width, back_bank):
+            blocks = width // P
+            turned = [bank(i, "turned%d_%d" % (t0, i)) for i in range(blocks)]
+            for r in range(terms):
+                z = weighted(r, t0, width)
+                for i in range(blocks):
+                    nc.tensor.matmul(
+                        turned[i][:, :P],
+                        lhsT=z[:, i * P : (i + 1) * P],
+                        rhs=ident[:],
+                        start=(r == 0),
+                        stop=(r == terms - 1),
+                        is_transpose=True,
+                    )
+            back = bank(back_bank, "back%d" % t0)
+            for i in range(blocks):
+                staged = keep.tile([P, P], F32, name="staged%d_%d" % (t0, i))
+                nc.scalar.copy(staged[:], turned[i][:, :P])
+                nc.tensor.transpose(back[:, i * P : (i + 1) * P], staged[:], ident[:])
+            return back
+
+        late = summed(TOP - 1, half, half, 4)
+        for c in range(half // CHUNK):
+            back = summed(TOP, c * CHUNK, CHUNK, 5 + c)
+            result = keep.tile([P, CHUNK], F32, name="result%d" % c)
+            nc.scalar.copy(result[:], back[:, :CHUNK])
+            nc.sync.dma_start(out=out[:, c * CHUNK : (c + 1) * CHUNK], in_=result[:])
+        last = [weighted(TOP - 1, half + c * CHUNK, CHUNK) for c in range(half // CHUNK)]
+        for c, z in enumerate(last):
+            result = keep.tile([P, CHUNK], F32, name="late_result%d" % c)
+            nc.vector.tensor_tensor(result[:], late[:, c * CHUNK : (c + 1) * CHUNK], z[:], ADD)
+            nc.sync.dma_start(out=out[:, half + c * CHUNK : half + (c + 1) * CHUNK], in_=result[:])

@@ -23,11 +23,12 @@ GELU = mybir.ActivationFunctionType.Gelu_apprx_tanh
 P = 128
 PACK = 4
 STRIPE = 16
-X_CHUNK = 256
-LAST_VECTOR_SHARE = 160
-WORD_LEAD = 2
-CHUNK = 256
-W_BYTES = PACK * N * 4
+X_CHUNKS = ((256, 160), (256, 160), (256, 160), (128, 0), (128, 80))
+W_LOAD = 2
+W_QUANT = 4
+WORD_GATHERS = (768, 768, 512)
+SCALE_GATHERS = (768, 512, 384, 256, 128)
+W_LOAD_BYTES = W_LOAD * PACK * N * 4
 
 
 def interleave(copy, grouped, raw, cols):
@@ -48,21 +49,23 @@ def tile_moe_ecr_lin_gelu_kernel(tc, xT, w, b, gate, offs, pos1, pos2, pos3, pos
             return psum.tile([P, 512], F32, name=name, tag="bank%d" % index)
 
         x_raw = []
-        for c in range(T // X_CHUNK):
-            raw = keep.tile([P, PACK, X_CHUNK], F32, name="x_raw%d" % c)
-            cols = slice(c * X_CHUNK, (c + 1) * X_CHUNK)
+        x_starts = [sum(width for width, share in X_CHUNKS[:c]) for c in range(len(X_CHUNKS))]
+        for c, (width, share) in enumerate(X_CHUNKS):
+            raw = keep.tile([P, PACK, width], F32, name="x_raw%d" % c)
+            cols = slice(x_starts[c], x_starts[c] + width)
             nc.sync.dma_start(out=raw[:], in_=xT[:, cols].rearrange("(p j) t -> p j t", j=PACK))
             x_raw.append(raw)
         offs_sb = keep.tile([P, SLOTS // STRIPE], U16, name="offs_sb")
         nc.sync.dma_start(offs_sb[:], offs)
         w_raw = []
-        for e in range(E):
-            raw = shared.tile([P, PACK, N], F32, name="w_raw%d" % e, offset=e * W_BYTES, align_bytes=64)
-            nc.sync.dma_start(out=raw[:], in_=w[e].rearrange("(p j) n -> p j n", j=PACK))
+        for u in range(E // W_LOAD):
+            raw = shared.tile([P, W_LOAD, PACK, N], F32, name="w_raw%d" % u, offset=u * W_LOAD_BYTES, align_bytes=64)
+            nc.sync.dma_start(
+                out=raw[:], in_=w[u * W_LOAD : (u + 1) * W_LOAD].rearrange("e (p j) n -> p e j n", j=PACK)
+            )
             w_raw.append(raw)
-            if e == 0:
-                bias = keep.tile([P, E], F32, name="bias")
-                nc.sync.dma_start(out=bias[:], in_=b)
+        bias = keep.tile([P, E], F32, name="bias")
+        nc.sync.dma_start(out=bias[:], in_=b)
         pos_sb = []
         gate_sb = []
         for r, pos in enumerate((pos1, pos2, pos3, pos4)):
@@ -70,9 +73,7 @@ def tile_moe_ecr_lin_gelu_kernel(tc, xT, w, b, gate, offs, pos1, pos2, pos3, pos
             nc.sync.dma_start(lst[:], pos)
             pos_sb.append(lst)
         half = T // 2
-        gate_parts = [(0, TOP - 1, half, half)]
-        gate_parts.extend((0, TOP, c * CHUNK, CHUNK) for c in range(half // CHUNK))
-        gate_parts.append((TOP - 1, TOP, half, half))
+        gate_parts = [(0, TOP, 0, half), (0, TOP, half, half)]
         for r0, r1, t0, width in gate_parts:
             g = keep.tile([P, r1 - r0, width], F32, name="gate_sb%d_%d" % (r0, t0))
             nc.sync.dma_start(out=g[:], in_=gate[r0:r1, :, t0 : t0 + width].rearrange("r n t -> n r t"))
@@ -93,61 +94,73 @@ def tile_moe_ecr_lin_gelu_kernel(tc, xT, w, b, gate, offs, pos1, pos2, pos3, pos
         make_identity(nc, ident[:])
 
         x_words = keep.tile([P, T], U32, name="x_words", align_bytes=64)
-        for c, raw in enumerate(x_raw):
-            grouped = keep.tile([P, X_CHUNK, PACK], BF16, name="x_bf%d" % c, align_bytes=64)
-            if c == len(x_raw) - 1:
-                interleave(nc.vector.tensor_copy, grouped, raw, slice(0, LAST_VECTOR_SHARE))
-                interleave(nc.scalar.copy, grouped, raw, slice(LAST_VECTOR_SHARE, X_CHUNK))
-            else:
-                interleave(nc.vector.tensor_copy, grouped, raw, slice(0, X_CHUNK))
-            cols = slice(c * X_CHUNK, (c + 1) * X_CHUNK)
+        for c, (width, share) in enumerate(X_CHUNKS):
+            grouped = keep.tile([P, width, PACK], BF16, name="x_bf%d" % c, align_bytes=64)
+            if share:
+                interleave(nc.vector.tensor_copy, grouped, x_raw[c], slice(0, share))
+            interleave(nc.scalar.copy, grouped, x_raw[c], slice(share, width))
+            cols = slice(x_starts[c], x_starts[c] + width)
             nc.vector.quantize_mx(
                 out=x_words[:, cols].bitcast(FP8X4),
                 scales=x_scales[:, cols],
                 in_=grouped[:].rearrange("p t j -> p (t j)"),
             )
 
-        def slot_offsets(e):
-            return offs_sb[:, e * C // STRIPE : (e + 1) * C // STRIPE]
+        def slot_offsets(s0, width):
+            return offs_sb[:, s0 // STRIPE : (s0 + width) // STRIPE]
 
-        def gather_words(e):
-            if e < WORD_LEAD:
-                words = keep.tile([P, C], U32, name="slot_words%d" % e, align_bytes=64)
-            else:
-                words = shared.tile(
-                    [P, C], U32, name="slot_words%d" % e, offset=(e - WORD_LEAD) * W_BYTES, align_bytes=64
+        w_bf = [
+            keep.tile([P, W_QUANT, N, PACK], BF16, name="w_bf%d" % q, align_bytes=64) for q in range(E // W_QUANT)
+        ]
+        for u, raw in enumerate(w_raw):
+            q, first = divmod(u * W_LOAD, W_QUANT)
+            nc.scalar.copy(
+                out=w_bf[q][:, first : first + W_LOAD].rearrange("p e (c i) j -> p e c j i", i=4),
+                in_=raw[:].rearrange("p e j (c i) -> p e c j i", i=4),
+            )
+
+        slot_words = keep.tile([P, SLOTS], U32, name="slot_words", align_bytes=64)
+        s0 = 0
+        for width in WORD_GATHERS:
+            nc.vector.tensor_copy(slot_words[:, s0 : s0 + width], x_words[:].indirect(slot_offsets(s0, width)))
+            s0 = s0 + width
+
+        w_words, w_scales = [], []
+        s0 = 0
+        passes = 0
+        for piece, width in enumerate(SCALE_GATHERS):
+            if piece < E // W_QUANT:
+                words = keep.tile([P, W_QUANT * N], U32, name="w_words%d" % piece, align_bytes=64)
+                scales = keep.tile([P, W_QUANT * N], U8, name="w_scales%d" % piece, align_bytes=64)
+                nc.vector.quantize_mx(
+                    out=words[:].bitcast(FP8X4),
+                    scales=scales[:],
+                    in_=w_bf[piece][:].rearrange("p e n j -> p (e n j)"),
                 )
-            nc.vector.tensor_copy(words[:], x_words[:].indirect(slot_offsets(e)))
-            return words
-
-        slot_words = [gather_words(e) for e in range(WORD_LEAD)]
-        for e in range(E):
-            grouped = keep.tile([P, N, PACK], BF16, name="w_bf%d" % e, align_bytes=64)
-            interleave(nc.scalar.copy, grouped, w_raw[e], slice(0, N))
-            w_words = keep.tile([P, N], U32, name="w_words%d" % e, align_bytes=64)
-            w_scales = keep.tile([P, N], U8, name="w_scales%d" % e, align_bytes=64)
-            nc.vector.quantize_mx(
-                out=w_words[:].bitcast(FP8X4),
-                scales=w_scales[:],
-                in_=grouped[:].rearrange("p n j -> p (n j)"),
-            )
+                w_words.append(words)
+                w_scales.append(scales)
+            host = (min(piece + 1, E // W_QUANT) * W_QUANT) // W_LOAD - 1
             slot_scales = shared.tile(
-                [P, C], U8, name="slot_scales%d" % e, offset=e * W_BYTES + 4 * C, align_bytes=64
+                [P, width], U8, name="slot_scales%d" % piece, offset=host * W_LOAD_BYTES + s0, align_bytes=64
             )
-            nc.vector.tensor_copy(slot_scales[:], x_scales[:].indirect(slot_offsets(e)))
-            if e + WORD_LEAD < E:
-                slot_words.append(gather_words(e + WORD_LEAD))
-            acc = bank(e, "acc%d" % e)
-            nc.tensor.matmul_mx(
-                out=acc[:, :C],
-                lhsT=w_words[:].bitcast(FP8X4),
-                lhsT_scale=w_scales[:],
-                rhs=slot_words[e][:].bitcast(FP8X4),
-                rhs_scale=slot_scales[:],
-                start=True,
-                stop=True,
-            )
-            nc.scalar.activation(y[:, e * C : (e + 1) * C], acc[:, :C], GELU, bias=bias[:, e : e + 1])
+            nc.vector.tensor_copy(slot_scales[:], x_scales[:].indirect(slot_offsets(s0, width)))
+            edges = sorted(set([s0, s0 + width] + [e * C for e in range(E) if s0 < e * C < s0 + width]))
+            for lo, hi in zip(edges, edges[1:]):
+                e = lo // C
+                q, w_cols = e // W_QUANT, slice((e % W_QUANT) * N, (e % W_QUANT + 1) * N)
+                acc = bank(passes % 8, "acc%d" % lo)
+                passes = passes + 1
+                nc.tensor.matmul_mx(
+                    out=acc[:, : hi - lo],
+                    lhsT=w_words[q][:, w_cols].bitcast(FP8X4),
+                    lhsT_scale=w_scales[q][:, w_cols],
+                    rhs=slot_words[:, lo:hi].bitcast(FP8X4),
+                    rhs_scale=slot_scales[:, lo - s0 : hi - s0],
+                    start=True,
+                    stop=True,
+                )
+                nc.scalar.activation(y[:, lo:hi], acc[:, : hi - lo], GELU, bias=bias[:, e : e + 1])
+            s0 = s0 + width
 
         def weighted(r, t0, width):
             z = keep.tile([P, width], F32, name="z%d_%d" % (r, t0))
@@ -155,35 +168,44 @@ def tile_moe_ecr_lin_gelu_kernel(tc, xT, w, b, gate, offs, pos1, pos2, pos3, pos
             nc.vector.tensor_tensor(z[:], y[:].indirect(offsets), gate_of(r, t0, width), MULT)
             return z
 
-        def summed(terms, t0, width, back_bank):
-            blocks = width // P
-            turned = [bank(i, "turned%d_%d" % (t0, i)) for i in range(blocks)]
-            for r in range(terms):
-                z = weighted(r, t0, width)
-                for i in range(blocks):
-                    nc.tensor.matmul(
-                        turned[i][:, :P],
-                        lhsT=z[:, i * P : (i + 1) * P],
-                        rhs=ident[:],
-                        start=(r == 0),
-                        stop=(r == terms - 1),
-                        is_transpose=True,
-                    )
+        def add_turned(turned, z, t0, width, start, stop):
+            for i in range(width // P):
+                nc.tensor.matmul(
+                    turned[(t0 % half) // P + i][:, :P],
+                    lhsT=z[:, i * P : (i + 1) * P],
+                    rhs=ident[:],
+                    start=start,
+                    stop=stop,
+                    is_transpose=True,
+                )
+
+        def turn_back(turned, t0, width, back_bank):
             back = bank(back_bank, "back%d" % t0)
-            for i in range(blocks):
+            for i in range(width // P):
                 staged = keep.tile([P, P], F32, name="staged%d_%d" % (t0, i))
-                nc.scalar.copy(staged[:], turned[i][:, :P])
+                nc.scalar.copy(staged[:], turned[(t0 % half) // P + i][:, :P])
                 nc.tensor.transpose(back[:, i * P : (i + 1) * P], staged[:], ident[:])
             return back
 
-        late = summed(TOP - 1, half, half, 4)
-        for c in range(half // CHUNK):
-            back = summed(TOP, c * CHUNK, CHUNK, 5 + c)
-            result = keep.tile([P, CHUNK], F32, name="result%d" % c)
-            nc.scalar.copy(result[:], back[:, :CHUNK])
-            nc.sync.dma_start(out=out[:, c * CHUNK : (c + 1) * CHUNK], in_=result[:])
-        last = [weighted(TOP - 1, half + c * CHUNK, CHUNK) for c in range(half // CHUNK)]
-        for c, z in enumerate(last):
-            result = keep.tile([P, CHUNK], F32, name="late_result%d" % c)
-            nc.vector.tensor_tensor(result[:], late[:, c * CHUNK : (c + 1) * CHUNK], z[:], ADD)
-            nc.sync.dma_start(out=out[:, half + c * CHUNK : half + (c + 1) * CHUNK], in_=result[:])
+        turned = [bank(i, "early_turned%d" % i) for i in range(half // P)]
+        for r in range(TOP):
+            add_turned(turned, weighted(r, 0, half), 0, half, r == 0, r == TOP - 1)
+        back = turn_back(turned, 0, half, 4)
+        result = keep.tile([P, half], F32, name="early_result")
+        nc.scalar.copy(result[:], back[:])
+        nc.sync.dma_start(out=out[:, :half], in_=result[:])
+
+        quarter = half // 2
+        late_starts = (half, half + quarter)
+        turned = [bank(i, "late_turned%d" % i) for i in range(half // P)]
+        for r in range(TOP - 2):
+            add_turned(turned, weighted(r, half, half), half, half, r == 0, False)
+        late = []
+        for c, t0 in enumerate(late_starts):
+            add_turned(turned, weighted(TOP - 2, t0, quarter), t0, quarter, False, True)
+            late.append(turn_back(turned, t0, quarter, 5 + c))
+        last = [weighted(TOP - 1, t0, quarter) for t0 in late_starts]
+        for c, t0 in enumerate(late_starts):
+            result = keep.tile([P, quarter], F32, name="late_result%d" % c)
+            nc.vector.tensor_tensor(result[:], late[c][:, :quarter], last[c][:], ADD)
+            nc.sync.dma_start(out=out[:, t0 : t0 + quarter], in_=result[:])

@@ -188,8 +188,8 @@ def tile_moe_ecr_lin_gelu_kernel(tc, xT, w, b, gate, offs, pos1, pos2, pos3, pos
             return back
 
         turned = [bank(i, "early_turned%d" % i) for i in range(half // P)]
-        for r in range(TOP):
-            add_turned(turned, weighted(r, 0, half), 0, half, r == 0, r == TOP - 1)
+        for r in reversed(range(TOP)):
+            add_turned(turned, weighted(r, 0, half), 0, half, r == TOP - 1, r == 0)
         back = turn_back(turned, 0, half, 4)
         result = keep.tile([P, half], F32, name="early_result")
         nc.scalar.copy(result[:], back[:])
@@ -198,13 +198,13 @@ def tile_moe_ecr_lin_gelu_kernel(tc, xT, w, b, gate, offs, pos1, pos2, pos3, pos
         quarter = half // 2
         late_starts = (half, half + quarter)
         turned = [bank(i, "late_turned%d" % i) for i in range(half // P)]
-        for r in range(TOP - 2):
-            add_turned(turned, weighted(r, half, half), half, half, r == 0, False)
+        for r in reversed(range(2, TOP)):
+            add_turned(turned, weighted(r, half, half), half, half, r == TOP - 1, False)
         late = []
         for c, t0 in enumerate(late_starts):
-            add_turned(turned, weighted(TOP - 2, t0, quarter), t0, quarter, False, True)
+            add_turned(turned, weighted(1, t0, quarter), t0, quarter, False, True)
             late.append(turn_back(turned, t0, quarter, 5 + c))
-        last = [weighted(TOP - 1, t0, quarter) for t0 in late_starts]
+        last = [weighted(0, t0, quarter) for t0 in late_starts]
         for c, t0 in enumerate(late_starts):
             result = keep.tile([P, quarter], F32, name="late_result%d" % c)
             nc.vector.tensor_tensor(result[:], late[c][:, :quarter], last[c][:], ADD)

from contextlib import ExitStack

import concourse.mybir as mybir
from concourse.masks import make_identity

K, T, E, C, N = 512, 1024, 8, 256, 128
TOP = 4
PAD = 64
SLOTS = E * C
FLOPS = 2 * K * N * SLOTS

F32 = mybir.dt.float32
BF16 = mybir.dt.bfloat16
I32 = mybir.dt.int32
U32 = mybir.dt.uint32
U16 = mybir.dt.uint16
U8 = mybir.dt.uint8
FP8X4 = mybir.dt.float8_e4m3fn_x4
MULT = mybir.AluOpType.mult
ADD = mybir.AluOpType.add
GELU = mybir.ActivationFunctionType.Gelu_apprx_tanh

P = 128
PACK = 4
STRIPE = 16
X_CHUNKS = ((256, 160), (256, 160), (256, 160), (128, 0), (128, 80))
W_LOAD = 2
W_QUANT = 4
WORD_GATHERS = (768, 768, 512)
SCALE_GATHERS = (768, 512, 384, 256, 128)
W_LOAD_BYTES = W_LOAD * PACK * N * 4


def interleave(copy, grouped, raw, cols):
    copy(
        out=grouped[:, cols, :].rearrange("p (c i) j -> p c j i", i=4),
        in_=raw[:, :, cols].rearrange("p j (c i) -> p c j i", i=4),
    )


def tile_moe_ecr_lin_gelu_kernel(tc, xT, w, b, gate, offs, pos1, pos2, pos3, pos4, out):
    nc = tc.nc
    with ExitStack() as ctx:
        keep = ctx.enter_context(tc.tile_pool(name="keep", bufs=1))
        shared = ctx.enter_context(tc.tile_pool(name="shared", bufs=1))
        psum = ctx.enter_context(tc.psum_pool(name="psum", bufs=1))

        def bank(index, name):
            return psum.tile([P, 512], F32, name=name, tag="bank%d" % index)

        x_raw = []
        x_starts = [sum(width for width, share in X_CHUNKS[:c]) for c in range(len(X_CHUNKS))]
        for c, (width, share) in enumerate(X_CHUNKS):
            raw = keep.tile([P, PACK, width], F32, name="x_raw%d" % c)
            cols = slice(x_starts[c], x_starts[c] + width)
            nc.sync.dma_start(out=raw[:], in_=xT[:, cols].rearrange("(p j) t -> p j t", j=PACK))
            x_raw.append(raw)
        offs_sb = keep.tile([P, SLOTS // STRIPE], U16, name="offs_sb")
        nc.sync.dma_start(offs_sb[:], offs)
        w_raw = []
        for u in range(E // W_LOAD):
            raw = shared.tile([P, W_LOAD, PACK, N], F32, name="w_raw%d" % u, offset=u * W_LOAD_BYTES, align_bytes=64)
            nc.sync.dma_start(
                out=raw[:], in_=w[u * W_LOAD : (u + 1) * W_LOAD].rearrange("e (p j) n -> p e j n", j=PACK)
            )
            w_raw.append(raw)
        bias = keep.tile([P, E], F32, name="bias")
        nc.sync.dma_start(out=bias[:], in_=b)
        pos_sb = []
        gate_sb = []
        for r, pos in enumerate((pos1, pos2, pos3, pos4)):
            lst = keep.tile([P, T // STRIPE], U16, name="pos_sb%d" % r)
            nc.sync.dma_start(lst[:], pos)
            pos_sb.append(lst)
        half = T // 2
        gate_parts = [(0, TOP, 0, half), (0, TOP, half, half)]
        for r0, r1, t0, width in gate_parts:
            g = keep.tile([P, r1 - r0, width], F32, name="gate_sb%d_%d" % (r0, t0))
            nc.sync.dma_start(out=g[:], in_=gate[r0:r1, :, t0 : t0 + width].rearrange("r n t -> n r t"))
            gate_sb.append(g)

        def gate_of(r, t0, width):
            for (r0, r1, g0, g_width), g in zip(gate_parts, gate_sb):
                if r0 <= r < r1 and g0 <= t0 < g0 + g_width:
                    return g[:, r - r0, t0 - g0 : t0 - g0 + width]

        x_scales = keep.tile([P, T], U8, name="x_scales", align_bytes=64)
        nc.vector.memset(x_scales[:].bitcast(I32), 0)
        zeros = keep.tile([P, PAD], F32, name="zeros")
        nc.vector.memset(zeros[:], 0.0)
        y = keep.tile([P, SLOTS + PAD], F32, name="y")
        nc.scalar.activation(y[:, SLOTS:], zeros[:], GELU)
        ident = keep.tile([P, P], F32, name="ident")
        make_identity(nc, ident[:])

        x_words = keep.tile([P, T], U32, name="x_words", align_bytes=64)
        for c, (width, share) in enumerate(X_CHUNKS):
            grouped = keep.tile([P, width, PACK], BF16, name="x_bf%d" % c, align_bytes=64)
            if share:
                interleave(nc.vector.tensor_copy, grouped, x_raw[c], slice(0, share))
            interleave(nc.scalar.copy, grouped, x_raw[c], slice(share, width))
            cols = slice(x_starts[c], x_starts[c] + width)
            nc.vector.quantize_mx(
                out=x_words[:, cols].bitcast(FP8X4),
                scales=x_scales[:, cols],
                in_=grouped[:].rearrange("p t j -> p (t j)"),
            )

        def slot_offsets(s0, width):
            return offs_sb[:, s0 // STRIPE : (s0 + width) // STRIPE]

        w_bf = [
            keep.tile([P, W_QUANT, N, PACK], BF16, name="w_bf%d" % q, align_bytes=64) for q in range(E // W_QUANT)
        ]
        for u, raw in enumerate(w_raw):
            q, first = divmod(u * W_LOAD, W_QUANT)
            nc.scalar.copy(
                out=w_bf[q][:, first : first + W_LOAD].rearrange("p e (c i) j -> p e c j i", i=4),
                in_=raw[:].rearrange("p e j (c i) -> p e c j i", i=4),
            )

        slot_words = keep.tile([P, SLOTS], U32, name="slot_words", align_bytes=64)
        s0 = 0
        for width in WORD_GATHERS:
            nc.vector.tensor_copy(slot_words[:, s0 : s0 + width], x_words[:].indirect(slot_offsets(s0, width)))
            s0 = s0 + width

        w_words, w_scales = [], []
        s0 = 0
        passes = 0
        for piece, width in enumerate(SCALE_GATHERS):
            if piece < E // W_QUANT:
                words = keep.tile([P, W_QUANT * N], U32, name="w_words%d" % piece, align_bytes=64)
                scales = keep.tile([P, W_QUANT * N], U8, name="w_scales%d" % piece, align_bytes=64)
                nc.vector.quantize_mx(
                    out=words[:].bitcast(FP8X4),
                    scales=scales[:],
                    in_=w_bf[piece][:].rearrange("p e n j -> p (e n j)"),
                )
                w_words.append(words)
                w_scales.append(scales)
            host = (min(piece + 1, E // W_QUANT) * W_QUANT) // W_LOAD - 1
            slot_scales = shared.tile(
                [P, width], U8, name="slot_scales%d" % piece, offset=host * W_LOAD_BYTES + s0, align_bytes=64
            )
            nc.vector.tensor_copy(slot_scales[:], x_scales[:].indirect(slot_offsets(s0, width)))
            edges = sorted(set([s0, s0 + width] + [e * C for e in range(E) if s0 < e * C < s0 + width]))
            for lo, hi in zip(edges, edges[1:]):
                e = lo // C
                q, w_cols = e // W_QUANT, slice((e % W_QUANT) * N, (e % W_QUANT + 1) * N)
                acc = bank(passes % 8, "acc%d" % lo)
                passes = passes + 1
                nc.tensor.matmul_mx(
                    out=acc[:, : hi - lo],
                    lhsT=w_words[q][:, w_cols].bitcast(FP8X4),
                    lhsT_scale=w_scales[q][:, w_cols],
                    rhs=slot_words[:, lo:hi].bitcast(FP8X4),
                    rhs_scale=slot_scales[:, lo - s0 : hi - s0],
                    start=True,
                    stop=True,
                )
                nc.scalar.activation(y[:, lo:hi], acc[:, : hi - lo], GELU, bias=bias[:, e : e + 1])
            s0 = s0 + width

        def weighted(r, t0, width):
            z = keep.tile([P, width], F32, name="z%d_%d" % (r, t0))
            offsets = pos_sb[r][:, t0 // STRIPE : (t0 + width) // STRIPE]
            nc.vector.tensor_tensor(z[:], y[:].indirect(offsets), gate_of(r, t0, width), MULT)
            return z

        def add_turned(turned, z, t0, width, start, stop):
            for i in range(width // P):
                nc.tensor.matmul(
                    turned[(t0 % half) // P + i][:, :P],
                    lhsT=z[:, i * P : (i + 1) * P],
                    rhs=ident[:],
                    start=start,
                    stop=stop,
                    is_transpose=True,
                )

        def turn_back(turned, t0, width, back_bank):
            back = bank(back_bank, "back%d" % t0)
            for i in range(width // P):
                staged = keep.tile([P, P], F32, name="staged%d_%d" % (t0, i))
                nc.scalar.copy(staged[:], turned[(t0 % half) // P + i][:, :P])
                nc.tensor.transpose(back[:, i * P : (i + 1) * P], staged[:], ident[:])
            return back

        turned = [bank(i, "early_turned%d" % i) for i in range(half // P)]
        for r in reversed(range(TOP)):
            add_turned(turned, weighted(r, 0, half), 0, half, r == TOP - 1, r == 0)
        back = turn_back(turned, 0, half, 4)
        result = keep.tile([P, half], F32, name="early_result")
        nc.scalar.copy(result[:], back[:])
        nc.sync.dma_start(out=out[:, :half], in_=result[:])

        quarter = half // 2
        late_starts = (half, half + quarter)
        turned = [bank(i, "late_turned%d" % i) for i in range(half // P)]
        for r in reversed(range(2, TOP)):
            add_turned(turned, weighted(r, half, half), half, half, r == TOP - 1, False)
        late = []
        for c, t0 in enumerate(late_starts):
            add_turned(turned, weighted(1, t0, quarter), t0, quarter, False, True)
            late.append(turn_back(turned, t0, quarter, 5 + c))
        last = [weighted(0, t0, quarter) for t0 in late_starts]
        for c, t0 in enumerate(late_starts):
            result = keep.tile([P, quarter], F32, name="late_result%d" % c)
            nc.vector.tensor_tensor(result[:], late[c][:, :quarter], last[c][:], ADD)
            nc.sync.dma_start(out=out[:, t0 : t0 + quarter], in_=result[:])
